import numpy as np, ml_dtypes
CORES = [144,200,272,328,400,456]
N = 6
import mx_ref
NC = 192
BF = ml_dtypes.bfloat16
def cut(t, i, w=512):
    return t[:, w * i:w * i + w]
def tile(rs):
    return np.stack(rs, axis=2).reshape(128, -1).astype(BF)
def onehot(t, r):
    own, p, b = t[:, :NC], t[:, NC:2 * NC], t[:, 2 * NC:]
    return tile([((own == r) & (p == np.arange(128)[:, None]) & (b == f)).astype(np.float32) for f in range(4)])
def setup_inputs(rng):
    def f(*shape):
        return mx_ref.flush((rng.standard_normal(shape, dtype=np.float32) * np.exp2(rng.integers(-2, 3, shape[:-1] + (1,)))).astype(BF))
    t = np.concatenate([rng.integers(0, N, (N, 1, NC)), rng.integers(0, 128, (N, 1, NC)), rng.integers(0, 4, (N, 1, NC))], axis=2)
    return {"tg": np.broadcast_to(t, (N, 128, 3 * NC)).astype(BF).copy(), "tab": f(N, 128, 4 * 512), "w": f(N, 128, 512)}
def setup_inputs_blocks(rng):
    d = setup_inputs(rng)
    for k in ("tab", "w"): d[k] = mx_ref.spread(d[k], rng, 4)
    return d
def setup_inputs_wide(rng):
    d = setup_inputs(rng)
    for k in ("tab", "w"): d[k] = mx_ref.flush((d[k].astype(np.float32) * np.exp2(rng.integers(-6, 7, (N, 1, 1))).astype(np.float32)).astype(BF))
    return d
def setup_inputs_hot(rng):
    d = setup_inputs(rng); t = d["tg"].astype(np.float32); t[:, :, :NC] = rng.integers(0, N); t[:, :, NC:2 * NC] = np.broadcast_to(rng.integers(0, 4, (N, 1, NC)), (N, 128, NC))
    d["tg"] = t.astype(BF)
    return d
def reference(tg, tab, w):
    y = np.zeros((N, 128, NC), np.float32)
    for j in range(N):
        qw = mx_ref.quantize(w[j])
        for r in range(N):
            o = mx_ref.quantize(onehot(tg[j].astype(np.float32), r))
            e = mx_ref.quantize(tile([mx_ref.matmul(mx_ref.quantize(cut(tab[r], f)), o) for f in range(4)]))
            p = mx_ref.matmul(qw, e)
            y[j] = p if r == 0 else y[j] + p
    return {"y": y}

from concourse.bass import DstId, RemoteDMATransfer
from concourse.mybir import dt, AluOpType, ActivationFunctionType

NR = 6
NC = 192
KC = 6
ZB = 7

SCRATCH = {
    "tgs": ("sbuf", [128, 3 * KC], "bfloat16"),
    "km": ("sbuf", [128, 12 * KC], "float32"),
    "key": ("sbuf", [128, KC], "bfloat16"),
    "rkey": ("sbuf", [128, KC], "bfloat16"),
    "land": ("sbuf", [128, NR * KC], "bfloat16"),
    "qf": ("sbuf", [128, 1], "float32"),
    "kcol": ("sbuf", [128, 4], "bfloat16"),
    "msk": ("sbuf", [128, 2 * NC], "bfloat16"),
    "d1": ("sbuf", [128, NR * NC], "bfloat16"),
    "rep": ("sbuf", [128, NR * NC], "bfloat16"),
    "kt": ("sbuf", [128, NR * NC], "bfloat16"),
    "o": ("sbuf", [128, NR * NC * 4], "bfloat16"),
    "oq": ("sbuf", [128, NR * NC], "float8_e4m3fn_x4"),
    "op": ("sbuf", [128, NR * NC], "uint8"),
    "e": ("sbuf", [128, NR * NC * 4], "bfloat16"),
    "eq": ("sbuf", [128, NR * NC], "float8_e4m3fn_x4"),
    "ep": ("sbuf", [128, NR * NC], "uint8"),
    "tabs": ("sbuf", [128, 2048], "bfloat16"),
    "tq": ("sbuf", [128, 512], "float8_e4m3fn_x4"),
    "tp": ("sbuf", [128, 512], "uint8"),
    "ws": ("sbuf", [128, 512], "bfloat16"),
    "wq": ("sbuf", [128, 128], "float8_e4m3fn_x4"),
    "wp": ("sbuf", [128, 128], "uint8"),
    "rq": ("sbuf", [128, NR * NC], "float8_e4m3fn_x4"),
    "rp": ("sbuf", [128, NR * NC], "uint8"),
    "xq": ("sbuf", [128, 2 * NC], "float8_e4m3fn_x4"),
    "xp": ("sbuf", [128, 2 * NC], "uint8"),
    "ysb": ("sbuf", [128, NC], "float32"),
    "ps": ("psum", [128, 512 * (ZB + 1)], "float32"),
}
SEMAPHORES = (["sent", "xk", "xc0", "xc1", "xs"]
              + ["k%d" % r for r in range(NR)] + ["e%d" % r for r in range(NR)]
              + ["tg", "tab0", "tab1", "wl", "io", "ms", "mz", "dz", "kk", "kl", "ks", "k_1", "k_2", "k_3", "key",
                 "tq0", "tq1", "wqd", "ym", "yc", "yd"]
              + ["%s_%d" % (s, t) for s in ("sc", "sn", "tr", "cm", "qo", "za", "zb", "qe") for t in range(NR)]
              + ["z_%d_%d" % (t, f) for t in range(NR) for f in range(4)])

_PLANS = {}


def _bits(m):
    return [1 << i for i in range(m.bit_length()) if (m >> i) & 1]


def _share(m, n):
    b = _bits(m)
    k = 1
    while 2 * k * n <= len(b):
        k *= 2
    return [sum(b[i * k:(i + 1) * k]) for i in range(n)]


def _plan(cores, topo):
    world = 4 * 128
    out = []
    for r in range(NR):
        c = cores[r]
        chipmates = [h for h in range(world) if h != c and topo.host(h) == topo.host(c) and topo.chip(h) == topo.chip(c)]
        others = [d for d in range(NR) if d != r]
        direct = [d for d in others if topo.may_write(c, cores[d])]
        rest = [d for d in others if d not in direct]
        chip = [d for d in rest if any(topo.may_write(h, cores[d]) for h in chipmates)]
        diag = [d for d in rest if d not in chip]
        relays = []
        if diag:
            busy = set(topo.host(x) for x in cores)
            cand = [x for x in range(world) if topo.host(x) not in busy and topo.chip(x) == topo.chip(c)
                    and topo.may_write(c, x) and all(topo.may_write(x, cores[d]) for d in diag)]
            crossing = topo.rack(topo.host(cand[0])) != topo.rack(topo.host(c))
            pick = [x for x in cand if (topo.die(x) != topo.die(c)) == crossing]
            diag.sort(key=lambda d: topo.chip(cores[d]) == topo.chip(c))
            relays.append((pick[0], diag, "diag"))
        own = [h for h in chipmates if topo.die(h) == topo.die(c) and all(topo.may_write(h, cores[d]) for d in chip)]
        far = [d for d in chip if topo.rack(topo.host(cores[d])) != topo.rack(topo.host(c))]
        near = [d for d in chip if d not in far]
        if len(chip) > 2:
            relays.append((own[1], far, "chip"))
            relays.append((own[0], sorted(near, key=lambda d: topo.host(cores[d]) == topo.host(c)), "chip"))
        else:
            relays.append((own[0], far + near, "chip"))
        late = [d for x in relays for d in x[1]]
        order = [r] + direct + late
        batches = [direct] + [late[i:i + 2] for i in range(0, len(late), 2)]
        off = topo.mask(c, cores[direct[0]])
        on = topo.mask(c, own[0]) & ~off
        first = [cores[d] for d in direct] + [x[0] for x in relays if x[2] == "diag"]
        onchip = [x[0] for x in relays if x[2] == "chip"]
        kmask = dict(zip(first, _share(off, len(first))))
        kmask.update(zip(onchip, _share(on, len(onchip))))
        emask = dict(zip([cores[d] for d in direct], _share(off, len(direct))))
        for x in relays:
            emask[x[0]] = off if x[2] == "diag" or (len(chip) > 2 and x[0] == own[1]) else on
        out.append({"direct": direct, "relays": relays, "order": order, "batches": batches, "kmask": kmask, "emask": emask,
                    "firsts": first + onchip})
    kn, en = {}, {}
    for r in range(NR):
        p = out[r]
        for d in p["direct"]:
            kn[d, r] = len(_bits(p["kmask"][cores[d]]))
            en[d, r] = 2 * len(_bits(p["emask"][cores[d]]))
        for x, ds, kind in p["relays"]:
            for i, d in enumerate(ds):
                m = topo.mask(x, cores[d])
                part = _share(m, len(ds))[i]
                kn[d, r] = len(_bits(part))
                en[d, r] = len(_bits(m)) + len(_bits(part))
    return {"ranks": out, "kn": kn, "en": en}


def _dst(topo, d, s):
    rid, pid = topo.addr(d, s)
    return DstId(rid=rid, pnc=pid)


def _send(g, topo, core, moves, T):
    if len(moves) == 1:
        d, m, sem, out, src = moves[0]
        rid, pid = topo.addr(d, core)
        g.remote_dma(out_ap=out, in_ap=src, remote_sem=sem, local_sem=T.sem["sent"], pid=pid, routing_id=rid,
                     dma_engine_mask=m)
    else:
        g.remote_dma_fused([RemoteDMATransfer(dst_ids=[_dst(topo, d, core)], dma_engine_mask=m, remote_sem=sem, src=src, dst=out)
                            for d, m, sem, out, src in moves], local_sem=T.sem["sent"])
    return sum(len(_bits(x[1])) for x in moves)


def _relay(g, core, T, topo, plan, r, ds):
    cores = T.cores
    p = plan["ranks"][r]
    full = [topo.mask(core, cores[d]) for d in ds]
    parts = [_share(full[i], len(ds))[i] for i in range(len(ds))]
    n = 0

    def slot(d):
        return plan["ranks"][d]["order"].index(r) - 1
    g.wait_ge(T.sem["xk"], len(_bits(p["kmask"][core])))
    n += _send(g, topo, core, [(cores[d], parts[i], T.sem["k%d" % r], T.land[:, KC * slot(d):KC * slot(d) + KC], T.rkey[:])
                               for i, d in enumerate(ds)], T)
    ne = len(_bits(p["emask"][core]))
    for i, d in enumerate(ds):
        g.wait_ge(T.sem["xc%d" % i], ne)
        n += _send(g, topo, core, [(cores[d], full[i], T.sem["e%d" % r], T.rq[:, NC * r:NC * r + NC].bitcast(dt.uint8),
                                    T.xq[:, NC * i:NC * i + NC].bitcast(dt.uint8))], T)
    g.wait_ge(T.sem["xs"], ne)
    n += _send(g, topo, core, [(cores[d], parts[i], T.sem["e%d" % r], T.rp[:, NC * r:NC * r + NC], T.xp[:, NC * i:NC * i + NC])
                               for i, d in enumerate(ds)], T)
    g.wait_ge(T.sem["sent"], n)


def rank_program(g, core, T, topo):
    if "p" not in _PLANS:
        _PLANS["p"] = _plan(T.cores, topo)
    plan = _PLANS["p"]
    rank = T.rank_of(core)
    if rank is None:
        for r in range(NR):
            for x, ds, kind in plan["ranks"][r]["relays"]:
                if x == core:
                    _relay(g, core, T, topo, plan, r, ds)
        return
    cores = T.cores
    me = plan["ranks"][rank]
    order = me["order"]
    V, S, X, Y = g.vector, g.scalar, g.tensor, g.sync
    A = AluOpType
    Copy, Ident = ActivationFunctionType.Copy, ActivationFunctionType.Identity
    cnt, seen = {}, set()

    def did(op, name, n=1):
        op.then_inc(T.sem[name], n)
        cnt[name] = cnt.get(name, 0) + n

    def need(q, tag, name):
        if (tag, name) not in seen:
            seen.add((tag, name))
            q.wait_ge(T.sem[name], cnt[name])
    for d in range(NR):
        if d != rank:
            cnt["k%d" % d] = plan["kn"][rank, d]
            cnt["e%d" % d] = plan["en"][rank, d]
    nsent = 0

    did(Y.dma_start(T.tgs[:, 0:KC], T.tg[0:4, 0:NC]), "tg", 16)
    did(S.dma_start(T.tgs[:, KC:2 * KC], T.tg[0:4, 2 * NC:3 * NC]), "tg", 16)
    did(Y.dma_start(T.tgs[:, 2 * KC:3 * KC], T.tg[0:4, NC:2 * NC]), "tg", 16)
    did(S.dma_start(T.tabs[:, 0:1024], T.tab[:, 0:1024]), "tab0", 16)
    did(Y.dma_start(T.tabs[:, 1024:2048], T.tab[:, 1024:2048]), "tab1", 16)
    did(Y.dma_start(T.ws[:], T.w[:]), "wl", 16)

    did(g.iota(T.qf[:], [[0, 1]], 128, 1, allow_small_or_imprecise_dtypes=True), "io")
    did(V.memset(T.msk[:], 1.0), "ms")
    did(V.memset(T.d1[:], 0.0), "dz")
    need(V, "V", "ms")
    did(V.memset(T.msk[:, 0:2 * NC:32], 0.0), "mz")
    need(V, "V", "io")
    for b in range(4):
        did(V.tensor_scalar(out=T.kcol[:, b:b + 1], in0=T.qf[:], scalar1=float(2.0 ** (6 * b + rank)), scalar2=None, op0=A.mult), "kk")

    own, bb, pp = T.tgs[:, 0:KC], T.tgs[:, KC:2 * KC], T.tgs[:, 2 * KC:3 * KC]

    def km(i):
        return T.km[:, KC * i:KC * i + KC]
    need(V, "V", "tg")
    need(S, "S", "tg")
    did(V.tensor_scalar(out=km(0), in0=bb, scalar1=63.0, scalar2=1.0, op0=A.mult, op1=A.add), "kl")
    did(V.tensor_scalar(out=km(1), in0=bb, scalar1=258048.0, scalar2=-512000.0, op0=A.mult, op1=A.add), "kl")
    did(V.tensor_scalar(out=km(2), in0=own, scalar1=1.0, scalar2=None, op0=A.add), "kl")
    did(S.activation(out=km(3), in_=own, func=Ident, bias=-4.0, scale=4.0), "ks")
    did(S.activation(out=km(4), in_=own, func=Ident, bias=-48.0, scale=16.0), "ks")
    did(S.activation(out=km(5), in_=pp, func=Ident, bias=128.0, scale=1.0), "ks")
    need(V, "V", "kl")
    did(V.tensor_tensor(out=km(6), in0=km(0), in1=km(1), op=A.max), "k_1")
    need(V, "V", "ks")
    did(V.tensor_tensor(out=km(7), in0=km(2), in1=km(3), op=A.max), "k_2")
    need(V, "V", "k_1")
    did(V.tensor_tensor(out=km(8), in0=km(5), in1=km(6), op=A.mult), "k_3")
    need(V, "V", "k_2")
    did(V.tensor_tensor(out=km(9), in0=km(7), in1=km(4), op=A.max), "k_3")
    need(V, "V", "k_3")
    did(V.tensor_tensor(out=T.key[:], in0=km(8), in1=km(9), op=A.mult), "key")

    need(g, "g", "key")
    moves = []
    for f in me["firsts"]:
        d = T.rank_of(f)
        if d is None:
            moves.append((f, me["kmask"][f], T.sem["xk"], T.rkey[:], T.key[:]))
        else:
            s = plan["ranks"][d]["order"].index(rank) - 1
            moves.append((f, me["kmask"][f], T.sem["k%d" % rank], T.land[:, KC * s:KC * s + KC], T.key[:]))
    nsent += _send(g, topo, core, moves, T)

    def prep(ts):
        a, n = ts[0], len(ts)
        for t in ts:
            need(V, "V", "key" if t == 0 else "k%d" % order[t])
        src = T.key[:] if a == 0 else T.land[:, KC * (a - 1):KC * (a - 1 + n)]
        need(V, "V", "dz")
        did(V.tensor_copy(T.d1[:, NC * a:NC * (a + n):32], src), "sc_%d" % a)
        need(V, "V", "sc_%d" % a)
        need(V, "V", "mz")
        did(V.tensor_tensor_scan(T.rep[:, NC * a:NC * (a + n)], T.msk[:, 0:NC * n], T.d1[:, NC * a:NC * (a + n)], 0.0,
                                 A.mult, A.add), "sn_%d" % a)
        need(V, "V", "sn_%d" % a)
        did(V.transpose(T.kt[:, NC * a:NC * (a + n)], T.rep[:, NC * a:NC * (a + n)]), "tr_%d" % a)
        return "tr_%d" % a

    def omake(t, tr):
        need(V, "V", tr)
        need(V, "V", "kk")
        for b in range(4):
            did(V.tensor_scalar(out=T.o[:, 4 * NC * t + b:4 * NC * (t + 1):4], in0=T.kt[:, NC * t:NC * (t + 1)],
                                scalar1=T.kcol[:, b:b + 1], scalar2=None, op0=A.is_equal), "cm_%d" % t)
        need(V, "V", "cm_%d" % t)
        did(V.quantize_mx(out=T.oq[:, NC * t:NC * (t + 1)], scales=T.op[:, NC * t:NC * (t + 1)],
                          in_=T.o[:, 4 * NC * t:4 * NC * (t + 1)]), "qo_%d" % t)

    def bank(t, f):
        i = 512 * ((4 * t + f) % ZB)
        return T.ps[:, i:i + NC]

    def zmm(t):
        need(X, "T", "qo_%d" % t)
        for f in range(4):
            need(X, "T", "tq%d" % (f // 2))
            k = 4 * t + f - ZB
            if k >= 0:
                need(X, "T", "%s_%d" % ("za" if k % 4 == 0 else "zb", k // 4))
            did(X.matmul_mx(bank(t, f), T.tq[:, 128 * f:128 * f + 128], T.tp[:, 128 * f:128 * f + 128],
                            T.oq[:, NC * t:NC * (t + 1)], T.op[:, NC * t:NC * (t + 1)], True, True), "z_%d_%d" % (t, f))

    def zcopy(t, vs=()):
        for f in range(4):
            out = T.e[:, 4 * NC * t + f:4 * NC * (t + 1):4]
            name = "%s_%d" % ("zb" if f else "za", t)
            if f in vs:
                need(V, "V", "z_%d_%d" % (t, f))
                did(V.tensor_copy(out, bank(t, f)), name)
            else:
                need(S, "S", "z_%d_%d" % (t, f))
                did(S.activation(out=out, in_=bank(t, f), func=Copy), name)

    def equant(t):
        need(V, "V", "za_%d" % t)
        need(V, "V", "zb_%d" % t)
        did(V.quantize_mx(out=T.eq[:, NC * t:NC * (t + 1)], scales=T.ep[:, NC * t:NC * (t + 1)],
                          in_=T.e[:, 4 * NC * t:4 * NC * (t + 1)]), "qe_%d" % t)

    def wmm(q, p, sem, start, stop):
        need(X, "T", sem)
        need(X, "T", "wqd")
        return X.matmul_mx(T.ps[:, 512 * ZB:512 * ZB + NC], T.wq[:], T.wp[:], q, p, start, stop)

    tr = prep([0])
    omake(0, tr)
    for h in range(2):
        need(V, "V", "tab%d" % h)
        did(V.quantize_mx(out=T.tq[:, 256 * h:256 * h + 256], scales=T.tp[:, 256 * h:256 * h + 256],
                          in_=T.tabs[:, 1024 * h:1024 * h + 1024]), "tq%d" % h)
    need(V, "V", "wl")
    did(V.quantize_mx(out=T.wq[:], scales=T.wp[:], in_=T.ws[:]), "wqd")
    zmm(0)
    zcopy(0)
    equant(0)
    wmm(T.eq[:, 0:NC], T.ep[:, 0:NC], "qe_0", True, False)

    nd = len(me["direct"])
    ts = list(range(1, 1 + nd))
    tr = prep(ts)
    for t in ts:
        omake(t, tr)
        zmm(t)
        zcopy(t)
    for t in ts:
        equant(t)
        need(g, "g", "qe_%d" % t)
    sem = T.sem["e%d" % rank]
    dc = [cores[d] for d in me["direct"]]
    nsent += _send(g, topo, core, [(c, me["emask"][c], sem, T.rq[:, NC * rank:NC * rank + NC].bitcast(dt.uint8),
                                    T.eq[:, NC * t:NC * t + NC].bitcast(dt.uint8)) for c, t in zip(dc, ts)], T)
    nsent += _send(g, topo, core, [(c, me["emask"][c], sem, T.rp[:, NC * rank:NC * rank + NC], T.ep[:, NC * t:NC * t + NC])
                                   for c, t in zip(dc, ts)], T)

    def send(t):
        n = 0
        for x, ds, kind in me["relays"]:
            if order[t] not in ds:
                continue
            i = ds.index(order[t])
            need(g, "g", "qe_%d" % t)
            n += _send(g, topo, core, [(x, me["emask"][x], T.sem["xc%d" % i], T.xq[:, NC * i:NC * i + NC].bitcast(dt.uint8),
                                        T.eq[:, NC * t:NC * t + NC].bitcast(dt.uint8))], T)
            if i + 1 == len(ds):
                n += _send(g, topo, core, [(x, me["emask"][x], T.sem["xs"], T.xp[:, 0:NC * len(ds)],
                                            T.ep[:, NC * (t - i):NC * (t + 1)])], T)
        return n
    late = list(range(1 + nd, NR))
    b2, b3 = late[:2], late[2:]
    tr2 = prep(b2)
    for t in b2:
        omake(t, tr2)
        zmm(t)
        zcopy(t)
    tr3 = prep(b3)
    for i in range(2):
        equant(b2[i])
        nsent += send(b2[i])
        if i < len(b3):
            t = b3[i]
            omake(t, tr3)
            zmm(t)
            if t != NR - 1:
                zcopy(t)
    for t in b3:
        if t == NR - 1:
            zcopy(t, (1, 3))
        equant(t)
        nsent += send(t)

    srcs = sorted([d for d in range(NR) if d != rank], key=lambda d: plan["ranks"][d]["order"].index(rank))
    for i, d in enumerate(srcs):
        op = wmm(T.rq[:, NC * d:NC * d + NC], T.rp[:, NC * d:NC * d + NC], "e%d" % d, False, i == len(srcs) - 1)
        if i == len(srcs) - 1:
            did(op, "ym")

    need(V, "V", "ym")
    for c in range(KC):
        did(V.tensor_copy(T.ysb[:, c:NC:KC], T.ps[:, 512 * ZB + 32 * c:512 * ZB + 32 * c + 32]), "yc")
    need(Y, "Y", "yc")
    did(Y.dma_start(T.y[:], T.ysb[:]), "yd", 16)
    need(Y, "Y", "yd")
    g.wait_ge(T.sem["sent"], nsent)
